import numpy as np
import ml_dtypes


def mxq(x, axis, fmt="e4m3"):
    dtype, down = {"e4m3": (ml_dtypes.float8_e4m3fn, 7), "e5m2": (ml_dtypes.float8_e5m2, 14)}[fmt]
    v = np.moveaxis(np.asarray(x, np.float32).astype(ml_dtypes.bfloat16).astype(np.float64), axis, -1)
    blocks = v.reshape(v.shape[:-1] + (-1, 32))
    amax = np.abs(blocks).max(-1, keepdims=True)
    byte = np.maximum(np.where(amax > 0, np.frexp(amax)[1] - 1 + 127, 0) - down, 1)
    scale = np.exp2(byte - 127.0)
    codes = (blocks / scale).astype(np.float32).astype(dtype).astype(np.float64)
    return np.moveaxis((codes * scale).reshape(v.shape), -1, axis)


WIDE = False


def mx_kscale(k):
    if not WIDE:
        return np.ones(k)
    levels = np.array([10, -10, 5, -5, 0])
    if k % 512:
        return np.exp2(np.random.permutation(np.resize(levels, k // 32))).repeat(32)
    a = np.empty((k // 512, 16))
    for p in range(k // 512):
        a[p, :8] = np.random.permutation(np.resize(levels, 8))
        for g in range(8):
            far = levels[np.abs(levels - a[p, g]) >= 10]
            a[p, g + 8] = far[np.random.randint(len(far))]
    return np.exp2(a.ravel()).repeat(32)


def f64(x):
    return np.asarray(x).astype(np.float64)


def striped(idx):
    return np.tile(idx.reshape(-1, 16).T, (8, 1)).astype(np.uint16)


def unstriped(offs):
    return offs[:16].T.reshape(-1).astype(np.int64)


def striped8(idx):
    return np.concatenate([x.reshape(-1, 16).T for x in idx]).astype(np.uint16)


def runs(offs, k):
    lists = np.stack([offs[16 * r : 16 * r + 16].T.reshape(-1) for r in range(8)]).astype(np.int64)
    return lists[np.arange(k) % 512 // 64]


def pack_weight(w):
    k, n = w.shape
    w = f64(np.asarray(w, np.float32).astype(ml_dtypes.bfloat16)).reshape(k // 32, 32, n)
    amax = np.abs(w).max(1)
    byte = np.clip(np.where(amax > 0, np.frexp(amax)[1] - 1 + 127 - 7, 1), 1, 254)
    scaled = (w * np.exp2(127.0 - byte)[:, None, :]).reshape(k, n).astype(np.float32)
    words = np.ascontiguousarray(scaled.reshape(k // 512, 128, 4, n).transpose(0, 1, 3, 2)).astype(ml_dtypes.float8_e4m3fn).view(np.uint8)
    return words, np.ascontiguousarray(byte.astype(np.uint8).reshape(k // 512, 16, n))


def unpack_weight(words, scales):
    g, p, n, _ = words.shape
    vals = np.ascontiguousarray(words).view(ml_dtypes.float8_e4m3fn).astype(np.float64) * np.repeat(np.exp2(scales.astype(np.float64) - 127.0), 8, axis=1)[..., None]
    return vals.transpose(0, 1, 3, 2).reshape(g * 512, n)


K, T, S, N, H, G, W, J = 512, 1024, 512, 512, 512, 2048, 256, 512


def setup_inputs():
    n = np.random.standard_normal
    s = mx_kscale(K)[:, None]
    u = mx_kscale(S)
    packed_xT = pack_weight(n((K, T)) * s)
    packed_dT = pack_weight(n((K, G)) / s)
    perm = np.stack([np.random.permutation(S) for _ in range(8)])
    return {
        "x_words": packed_xT[0],
        "x_scales": packed_xT[1],
        "w1": (n((K, H)) / np.sqrt(K) / s).astype(np.float32),
        "d_words": packed_dT[0],
        "d_scales": packed_dT[1],
        "tab": n((H, J)).astype(np.float32),
        "gn": (np.random.uniform(0.5, 1.5, (H, 1)) * u[:, None]).astype(np.float32),
        "gk": (np.random.uniform(0.5, 1.5, (H, 1)) * u[:, None]).astype(np.float32),
        "w2": (n((H, N)) / np.sqrt(2 * H) / u[:, None]).astype(np.float32),
        "w3": (n((H, N)) / np.sqrt(2 * H) / u[:, None]).astype(np.float32),
        "offs": striped(np.random.permutation(T)[:S]),
        "kidx": striped8(np.random.randint(0, G, (8, H))),
        "two": striped(np.random.permutation(T)[:S]),
        "n1": striped8(perm[:, :W]),
        "n2": striped8(perm[:, W:]),
        "n3": striped8(np.random.randint(0, J, (8, S))),
        "n4": striped8(np.random.randint(0, J, (8, S))),
        "n5": striped8(np.stack([np.random.permutation(S) for _ in range(8)])),
        "n6": striped(np.random.permutation(S)),
    }


def reference(x_words, x_scales, w1, d_words, d_scales, tab, gn, gk, w2, w3, offs, kidx, two, n1, n2, n3, n4, n5, n6):
    xq = unpack_weight(x_words, x_scales)[:, unstriped(offs)]
    y = mxq(f64(w1), 0, "e4m3").T @ xq
    pa = y[np.arange(H)[:, None], runs(n1, H)]
    pb = y[np.arange(H)[:, None], runs(n2, H)]
    rb = pa * pb
    ra = pa + pb
    ds = np.zeros((H, S))
    ds[np.arange(H)[:, None], runs(n1, H)] = ra
    dt = ds.copy()
    dt[np.arange(H)[:, None], runs(n2, H)] = rb
    z = f64(gn) * dt
    d_kidx = unpack_weight(d_words, d_scales)[np.arange(K)[:, None], runs(kidx, K)]
    x_two = unpack_weight(x_words, x_scales)[:, unstriped(two)]
    s = 0.0625 * (d_kidx.T @ x_two)
    z2 = f64(gk) * ((s[np.arange(H)[:, None], runs(n5, H)]) * (f64(tab)[np.arange(H)[:, None], runs(n3, H)]) + f64(tab)[np.arange(H)[:, None], runs(n4, H)])
    h = mxq(f64(w2), 0, "e4m3").T @ mxq(z, 0, "e4m3") + mxq(f64(w3), 0, "e4m3").T @ mxq(z2, 0, "e4m3")
    pa2 = h[:, unstriped(n6)]
    return (2.0 * (h * pa2)) / ((h) ** 2 + (pa2) ** 2 + 0.5)

@@ -1,0 +1,223 @@
+from contextlib import ExitStack
+
+import concourse.mybir as mybir
+
+K, T, S, N, H, G, W, J = 512, 1024, 512, 512, 512, 2048, 256, 512
+FLOPS = 4 * 2 * 512 * 512 * 512
+
+F32 = mybir.dt.float32
+BF16 = mybir.dt.bfloat16
+I32 = mybir.dt.int32
+U32 = mybir.dt.uint32
+U16 = mybir.dt.uint16
+U8 = mybir.dt.uint8
+FP8X4 = mybir.dt.float8_e4m3fn_x4
+ALU = mybir.AluOpType
+ACT = mybir.ActivationFunctionType
+P = 128
+PACK = 4
+HALF = 256
+T3_ON_SCALAR = 2
+
+
+def tile_picked_jkeybondkindaharm_none_p_kernel(tc, x_words, x_scales, w1, d_words, d_scales, tab, gn, gk, w2, w3, offs, kidx, two, n1, n2, n3, n4, n5, n6, out):
+    nc = tc.nc
+    with ExitStack() as ctx:
+        lists = ctx.enter_context(tc.tile_pool(name="lists", bufs=1))
+        keep = ctx.enter_context(tc.tile_pool(name="keep", bufs=1))
+        psum = ctx.enter_context(tc.psum_pool(name="psum", bufs=1))
+
+        def load_list(name, src):
+            tl = lists.tile(list(src.shape), U16, name=name)
+            nc.sync.dma_start(out=tl[:], in_=src)
+            return tl
+
+        def sb(name, shape, dtype, tag=None):
+            return keep.tile(shape, dtype, name=name, tag=tag or name, align_bytes=64)
+
+        def halves(lst):
+            return [(slice(h * HALF, (h + 1) * HALF), lst[:, h * 16:(h + 1) * 16]) for h in range(2)]
+
+        def mx(acc, lw, ls, rw, rs, start, stop):
+            nc.tensor.matmul_mx(out=acc, lhsT=lw.bitcast(FP8X4), lhsT_scale=ls, rhs=rw.bitcast(FP8X4), rhs_scale=rs, start=start, stop=stop)
+
+        def quant(name, grouped):
+            words = sb(name + "_w", [P, 512], U32)
+            scales = sb(name + "_s", [P, 512], U8)
+            nc.vector.quantize_mx(out=words[:].bitcast(FP8X4), scales=scales[:], in_=grouped[:])
+            return words, scales
+
+        xs = sb("xs", [P, T], U8)
+        dsc = sb("dsc", [P, G], U8)
+        nc.vector.memset(xs[:].bitcast(I32), 0)
+        nc.vector.memset(dsc[:].bitcast(I32), 0)
+        gk_sb = sb("gk_sb", [P, PACK], F32)
+        nc.gpsimd.dma_start(out=gk_sb[:], in_=gk.rearrange("(p t) o -> p (t o)", t=PACK))
+        gn_sb = sb("gn_sb", [P, PACK], F32)
+        nc.gpsimd.dma_start(out=gn_sb[:], in_=gn.rearrange("(p t) o -> p (t o)", t=PACK))
+        offs_l = load_list("offs_l", offs)
+        xw = sb("xw", [P, T], U32)
+        nc.sync.dma_start(out=xw[:].bitcast(I32), in_=x_words[0].rearrange("p n r -> p (n r)").bitcast(I32))
+        w1_rows = w1.rearrange("(p j) c -> p j c", j=PACK)
+        w1_raw = [sb("w1_raw%d" % h, [P, PACK, HALF], F32) for h in range(2)]
+        nc.sync.dma_start(out=w1_raw[0][:], in_=w1_rows[:, :, 0:HALF])
+        for q in range(4):
+            nc.sync.dma_start(out=xs[32 * q:32 * q + 4, :].bitcast(I32), in_=x_scales[0, 4 * q:4 * q + 4, :].bitcast(I32))
+        nc.sync.dma_start(out=w1_raw[1][:], in_=w1_rows[:, :, HALF:2 * HALF])
+        two_l = load_list("two_l", two)
+        n4_l = load_list("n4_l", n4)
+        tab_rows = tab.rearrange("(p t) c -> p t c", t=PACK)
+        tab_raw = [sb("tab_raw%d" % t, [P, J], F32) for t in range(PACK)]
+        nc.sync.dma_start(out=tab_raw[0][:], in_=tab_rows[:, 0, :])
+        kidx_l = load_list("kidx_l", kidx)
+        d_rows = d_scales[0].rearrange("(g e) c -> e g c", e=2)
+        for e in range(2):
+            nc.sync.dma_start(out=dsc[e:P:16, :].bitcast(I32), in_=d_rows[e].bitcast(I32))
+        dw = sb("dw", [P, G], U32)
+        nc.sync.dma_start(out=dw[:].bitcast(I32), in_=d_words[0].rearrange("p n r -> p (n r)").bitcast(I32))
+        n1_l = load_list("n1_l", n1)
+        n2_l = load_list("n2_l", n2)
+        for t in (1, 2, 3):
+            nc.sync.dma_start(out=tab_raw[t][:], in_=tab_rows[:, t, :])
+        n3_l = load_list("n3_l", n3)
+        n5_l = load_list("n5_l", n5)
+        w_raw = [sb("w_raw%d" % i, [P, PACK, N], F32) for i in range(2)]
+        for i, w in enumerate((w2, w3)):
+            nc.sync.dma_start(out=w_raw[i][:], in_=w.rearrange("(p j) c -> p j c", j=PACK))
+        n6_l = load_list("n6_l", n6)
+
+        gtab = [sb("gtab%d" % t, [P, J], F32) for t in range(PACK)]
+        t4 = sb("t4", [P, PACK, S], F32)
+
+        def tab_stage(t):
+            nc.scalar.activation(out=gtab[t][:], in_=tab_raw[t][:], func=ACT.Copy, scale=gk_sb[:, t:t + 1])
+            for cols, lst in halves(n4_l):
+                nc.scalar.activation(out=t4[:, t, cols], in_=gtab[t][:].indirect(lst), func=ACT.Copy)
+
+        xq_w = sb("xq_w", [P, S], U32)
+        xq_s = sb("xq_s", [P, S], U8)
+        x2_w = sb("x2_w", [P, S], U32)
+        x2_s = sb("x2_s", [P, S], U8)
+        nc.vector.tensor_copy(out=xq_w[:], in_=xw[:].indirect(offs_l[:]))
+        nc.vector.tensor_copy(out=xq_s[:], in_=xs[:].indirect(offs_l[:]))
+        w1_g = sb("w1_g", [P, PACK * H], BF16)
+        for h in range(2):
+            nc.scalar.copy(out=w1_g[:].rearrange("p (t m j) -> p m j t", t=PACK, j=PACK)[:, 64 * h:64 * (h + 1)],
+                           in_=w1_raw[h][:].rearrange("p j (m t) -> p m j t", t=PACK))
+        w1_w, w1_s = quant("w1", w1_g)
+        y_ps = [psum.tile([P, S], F32, name="bank%d" % t) for t in range(PACK)]
+        for t in range(PACK):
+            cols = slice(t * P, (t + 1) * P)
+            mx(y_ps[t][:], w1_w[:, cols], w1_s[:, cols], xq_w[:], xq_s[:], True, True)
+        dk_w = sb("dk_w", [P, H], U32, tag="dt0")
+        dk_s = sb("dk_s", [P, H], U8, tag="dt1")
+        key_w = sb("key_w", [P, H], U32)
+        key_s = sb("key_s", [P, H], U8)
+        nc.vector.tensor_copy(out=dk_s[:], in_=dsc[:].indirect(kidx_l[:]))
+        nc.vector.tensor_copy(out=key_s[:].rearrange("p (t m) -> p m t", t=PACK), in_=dk_s[:].rearrange("p (m t) -> p m t", t=PACK))
+        for e in range(2):
+            nc.sync.dma_start(out=key_s[2 + e:P:32, :].bitcast(I32), in_=key_s[16 + e:P:32, :].bitcast(I32))
+        nc.vector.tensor_copy(out=x2_w[:], in_=xw[:].indirect(two_l[:]))
+        nc.vector.tensor_copy(out=x2_s[:], in_=xs[:].indirect(two_l[:]))
+        nc.vector.tensor_copy(out=dk_w[:], in_=dw[:].indirect(kidx_l[:]))
+        nc.vector.tensor_copy(out=key_w[:].bitcast(I32).rearrange("p (t m) -> p m t", t=PACK), in_=dk_w[:].bitcast(I32).rearrange("p (m t) -> p m t", t=PACK))
+        s_ps = [psum.tile([P, S], F32, name="bank%d" % (PACK + t)) for t in range(PACK)]
+        for t in range(PACK):
+            cols = slice(t * P, (t + 1) * P)
+            mx(s_ps[t][:], key_w[:, cols], key_s[:, cols], x2_w[:], x2_s[:], True, True)
+
+        z_pl = sb("z_pl", [P, PACK, S], BF16)
+        dts = []
+
+        def z_scale(t):
+            nc.vector.tensor_scalar(out=z_pl[:, t, :], in0=dts[t][:], scalar1=gn_sb[:, t:t + 1], scalar2=None, op0=ALU.mult)
+
+        for t in range(PACK):
+            y_sb = sb("y_sb%d" % t, [P, S], F32)
+            nc.scalar.copy(out=y_sb[:], in_=y_ps[t][:])
+            pa = sb("pa%d" % t, [P, W], F32)
+            pb = sb("pb%d" % t, [P, W], F32)
+            nc.scalar.activation(out=pa[:], in_=y_sb[:].indirect(n1_l[:]), func=ACT.Copy)
+            nc.scalar.activation(out=pb[:], in_=y_sb[:].indirect(n2_l[:]), func=ACT.Copy)
+            dt = sb("dt%d" % t, [P, S], F32)
+            nc.vector.tensor_tensor(out=dt[:].indirect(n1_l[:]), in0=pa[:], in1=pb[:], op=ALU.add)
+            if t > 0:
+                z_scale(t - 1)
+            nc.vector.tensor_tensor(out=dt[:].indirect(n2_l[:]), in0=pa[:], in1=pb[:], op=ALU.mult)
+            dts.append(dt)
+        for t in range(PACK):
+            tab_stage(t)
+        st = sb("st", [P, PACK, S], F32)
+        for t in range(PACK):
+            s_sb = sb("s_sb%d" % t, [P, S], F32)
+            nc.scalar.mul(out=s_sb[:], in_=s_ps[t][:], mul=0.0625)
+            s5 = sb("s5_%d" % t, [P, S], F32)
+            for cols, lst in halves(n5_l):
+                nc.scalar.activation(out=s5[:, cols], in_=s_sb[:].indirect(lst), func=ACT.Copy)
+            if t < T3_ON_SCALAR:
+                t3 = sb("t3_%d" % t, [P, S], F32)
+                for cols, lst in halves(n3_l):
+                    nc.scalar.activation(out=t3[:, cols], in_=gtab[t][:].indirect(lst), func=ACT.Copy)
+                nc.vector.tensor_tensor(out=st[:, t, :], in0=t3[:], in1=s5[:], op=ALU.mult)
+            else:
+                for cols, lst in halves(n3_l):
+                    nc.vector.tensor_tensor(out=st[:, t, cols], in0=gtab[t][:].indirect(lst), in1=s5[:, cols], op=ALU.mult)
+            if t == 0:
+                z_scale(PACK - 1)
+        w_g = []
+        for i in range(2):
+            w_g.append(sb("w_g%d" % i, [P, PACK * N], BF16, tag="s_sb%d" % (2 + i)))
+            nc.scalar.copy(out=w_g[i][:].rearrange("p (c i j) -> p c j i", i=4, j=PACK), in_=w_raw[i][:].rearrange("p j (c i) -> p c j i", i=4))
+
+        z_g = sb("z_g", [P, PACK * S], BF16)
+        nc.vector.tensor_copy(out=z_g[:].rearrange("p (c i t) -> p c t i", i=4, t=PACK), in_=z_pl[:].rearrange("p t (c i) -> p c t i", i=4))
+        z2_g = sb("z2_g", [P, PACK * S], BF16)
+        nc.vector.tensor_tensor(out=z2_g[:].rearrange("p (c i t) -> p c t i", i=4, t=PACK),
+                                in0=st[:].rearrange("p t (c i) -> p c t i", i=4),
+                                in1=t4[:].rearrange("p t (c i) -> p c t i", i=4), op=ALU.add)
+        z_w, z_s = quant("z", z_g)
+        w2_w, w2_s = quant("w2", w_g[0])
+        z2_w, z2_s = quant("z2", z2_g)
+        w3_w, w3_s = quant("w3", w_g[1])
+
+        h_ps = [psum.tile([P, S], F32, name="bank%d" % mt) for mt in range(PACK)]
+        for mt in range(PACK):
+            cols = slice(mt * P, (mt + 1) * P)
+            mx(h_ps[mt][:], w2_w[:, cols], w2_s[:, cols], z_w[:], z_s[:], True, False)
+        for mt in range(PACK):
+            cols = slice(mt * P, (mt + 1) * P)
+            mx(h_ps[mt][:], w3_w[:, cols], w3_s[:, cols], z2_w[:], z2_s[:], False, True)
+        h_sb = [sb("h_sb%d" % mt, [P, S], F32, tag="y_sb%d" % mt) for mt in range(PACK)]
+        hh = [sb("hh%d" % mt, [P, S], F32, tag="s_sb%d" % mt) for mt in range(PACK)]
+        pa2 = [sb("pa2_%d" % mt, [P, S], F32, tag="dt%d" % mt) for mt in range(PACK)]
+        pp = [sb("pp%d" % mt, [P, S], F32, tag="s5_%d" % mt) for mt in range(PACK)]
+        num = [sb("num%d" % mt, [P, S], F32, tag="gtab%d" % mt) for mt in range(PACK)]
+        ssq = [sb("ssq%d" % mt, [P, S], F32, tag="tab_raw%d" % mt) for mt in range(PACK)]
+        root = [sb("root%d" % mt, [P, S], F32) for mt in range(PACK)]
+        rec = [sb("rec%d" % mt, [P, S], F32) for mt in range(PACK)]
+        res = [sb("res%d" % mt, [P, S], F32) for mt in range(PACK)]
+
+        def stage_a(mt):
+            nc.scalar.copy(out=h_sb[mt][:], in_=h_ps[mt][:])
+            nc.scalar.activation(out=hh[mt][:], in_=h_ps[mt][:], func=ACT.Square)
+            for c2, lst in halves(n6_l):
+                nc.vector.tensor_copy(out=pa2[mt][:, c2], in_=h_sb[mt][:].indirect(lst))
+
+        def stage_b(mt):
+            nc.scalar.activation(out=pp[mt][:], in_=pa2[mt][:], func=ACT.Square)
+            nc.vector.tensor_tensor(out=num[mt][:], in0=h_sb[mt][:], in1=pa2[mt][:], op=ALU.mult)
+            nc.vector.scalar_tensor_tensor(out=ssq[mt][:], in0=pp[mt][:], scalar=0.5, in1=hh[mt][:], op0=ALU.add, op1=ALU.add)
+
+        def stage_c(mt):
+            nc.scalar.activation(out=root[mt][:], in_=ssq[mt][:], func=ACT.Abs_reciprocal_sqrt)
+            nc.scalar.activation(out=rec[mt][:], in_=root[mt][:], func=ACT.Square)
+            nc.vector.scalar_tensor_tensor(out=res[mt][:], in0=num[mt][:], scalar=2.0, in1=rec[mt][:], op0=ALU.mult, op1=ALU.mult)
+            nc.sync.dma_start(out=out[mt * P:(mt + 1) * P, :], in_=res[mt][:])
+
+        for step in range(PACK + 2):
+            if step < PACK:
+                stage_a(step)
+            if 1 <= step <= PACK:
+                stage_b(step - 1)
+            if step >= 2:
+                stage_c(step - 2)

@@ -17,7 +17,7 @@ ACT = mybir.ActivationFunctionType
 P = 128
 PACK = 4
 HALF = 256
-T3_ON_SCALAR = 2
+T3_ON_SCALAR = 4
 
 
 def tile_picked_jkeybondkindaharm_none_p_kernel(tc, x_words, x_scales, w1, d_words, d_scales, tab, gn, gk, w2, w3, offs, kidx, two, n1, n2, n3, n4, n5, n6, out):
@@ -41,84 +41,100 @@ def tile_picked_jkeybondkindaharm_none_p_kernel(tc, x_words, x_scales, w1, d_wor
         def mx(acc, lw, ls, rw, rs, start, stop):
             nc.tensor.matmul_mx(out=acc, lhsT=lw.bitcast(FP8X4), lhsT_scale=ls, rhs=rw.bitcast(FP8X4), rhs_scale=rs, start=start, stop=stop)
 
-        def quant(name, grouped):
-            words = sb(name + "_w", [P, 512], U32)
-            scales = sb(name + "_s", [P, 512], U8)
+        def quant(name, grouped, width=512, tag=None):
+            words = sb(name + "_w", [P, width], U32, tag=tag)
+            scales = sb(name + "_s", [P, width], U8)
             nc.vector.quantize_mx(out=words[:].bitcast(FP8X4), scales=scales[:], in_=grouped[:])
             return words, scales
 
         xs = sb("xs", [P, T], U8)
         dsc = sb("dsc", [P, G], U8)
+        warm_in = sb("warm_in", [P, 1], F32)
+        warm_out = sb("warm_out", [P, 1], F32)
+        nc.vector.memset(warm_in[:], 1.0)
+        nc.scalar.activation(out=warm_out[:], in_=warm_in[:], func=ACT.Abs_reciprocal_sqrt)
         nc.vector.memset(xs[:].bitcast(I32), 0)
         nc.vector.memset(dsc[:].bitcast(I32), 0)
         gk_sb = sb("gk_sb", [P, PACK], F32)
-        nc.gpsimd.dma_start(out=gk_sb[:], in_=gk.rearrange("(p t) o -> p (t o)", t=PACK))
-        gn_sb = sb("gn_sb", [P, PACK], F32)
-        nc.gpsimd.dma_start(out=gn_sb[:], in_=gn.rearrange("(p t) o -> p (t o)", t=PACK))
-        offs_l = load_list("offs_l", offs)
-        xw = sb("xw", [P, T], U32)
-        nc.sync.dma_start(out=xw[:].bitcast(I32), in_=x_words[0].rearrange("p n r -> p (n r)").bitcast(I32))
-        w1_rows = w1.rearrange("(p j) c -> p j c", j=PACK)
-        w1_raw = [sb("w1_raw%d" % h, [P, PACK, HALF], F32) for h in range(2)]
-        nc.sync.dma_start(out=w1_raw[0][:], in_=w1_rows[:, :, 0:HALF])
-        for q in range(4):
-            nc.sync.dma_start(out=xs[32 * q:32 * q + 4, :].bitcast(I32), in_=x_scales[0, 4 * q:4 * q + 4, :].bitcast(I32))
-        nc.sync.dma_start(out=w1_raw[1][:], in_=w1_rows[:, :, HALF:2 * HALF])
-        two_l = load_list("two_l", two)
-        n4_l = load_list("n4_l", n4)
+        nc.sync.dma_start(out=gk_sb[:], in_=gk.rearrange("(p t) o -> p (t o)", t=PACK))
         tab_rows = tab.rearrange("(p t) c -> p t c", t=PACK)
         tab_raw = [sb("tab_raw%d" % t, [P, J], F32) for t in range(PACK)]
         nc.sync.dma_start(out=tab_raw[0][:], in_=tab_rows[:, 0, :])
+        n4_l = load_list("n4_l", n4)
+        n3_l = load_list("n3_l", n3)
+        offs_l = load_list("offs_l", offs)
+        xw = sb("xw", [P, T], U32)
+        nc.sync.dma_start(out=xw[:].bitcast(I32), in_=x_words[0].rearrange("p n r -> p (n r)").bitcast(I32))
+        two_l = load_list("two_l", two)
+        w1_raw = sb("w1_raw", [P, PACK, H], F32)
+        nc.sync.dma_start(out=w1_raw[:], in_=w1.rearrange("(p j) c -> p j c", j=PACK))
+        for q in range(4):
+            nc.sync.dma_start(out=xs[32 * q:32 * q + 4, :].bitcast(I32), in_=x_scales[0, 4 * q:4 * q + 4, :].bitcast(I32))
         kidx_l = load_list("kidx_l", kidx)
-        d_rows = d_scales[0].rearrange("(g e) c -> e g c", e=2)
-        for e in range(2):
-            nc.sync.dma_start(out=dsc[e:P:16, :].bitcast(I32), in_=d_rows[e].bitcast(I32))
+        nc.sync.dma_start(out=tab_raw[1][:], in_=tab_rows[:, 1, :])
         dw = sb("dw", [P, G], U32)
         nc.sync.dma_start(out=dw[:].bitcast(I32), in_=d_words[0].rearrange("p n r -> p (n r)").bitcast(I32))
         n1_l = load_list("n1_l", n1)
         n2_l = load_list("n2_l", n2)
-        for t in (1, 2, 3):
+        d_rows = d_scales[0].rearrange("(g e) c -> e g c", e=2)
+        for e in range(2):
+            nc.sync.dma_start(out=dsc[e:P:16, :].bitcast(I32), in_=d_rows[e].bitcast(I32))
+        for t in (2, 3):
             nc.sync.dma_start(out=tab_raw[t][:], in_=tab_rows[:, t, :])
-        n3_l = load_list("n3_l", n3)
         n5_l = load_list("n5_l", n5)
+        gn_sb = sb("gn_sb", [P, PACK], F32)
+        nc.sync.dma_start(out=gn_sb[:], in_=gn.rearrange("(p t) o -> p (t o)", t=PACK))
         w_raw = [sb("w_raw%d" % i, [P, PACK, N], F32) for i in range(2)]
         for i, w in enumerate((w2, w3)):
             nc.sync.dma_start(out=w_raw[i][:], in_=w.rearrange("(p j) c -> p j c", j=PACK))
         n6_l = load_list("n6_l", n6)
 
-        gtab = [sb("gtab%d" % t, [P, J], F32) for t in range(PACK)]
+        gtab = {}
         t4 = sb("t4", [P, PACK, S], F32)
+        t3 = {}
 
-        def tab_stage(t):
+        def tab_stage(t, tag=None):
+            gtab[t] = sb("gtab%d" % t, [P, J], F32, tag=tag)
             nc.scalar.activation(out=gtab[t][:], in_=tab_raw[t][:], func=ACT.Copy, scale=gk_sb[:, t:t + 1])
             for cols, lst in halves(n4_l):
                 nc.scalar.activation(out=t4[:, t, cols], in_=gtab[t][:].indirect(lst), func=ACT.Copy)
 
+        def t3_stage(t, tag=None):
+            if t < T3_ON_SCALAR:
+                t3[t] = sb("t3_%d" % t, [P, S], F32, tag=tag)
+                for cols, lst in halves(n3_l):
+                    nc.scalar.activation(out=t3[t][:, cols], in_=tab_raw[t][:].indirect(lst), func=ACT.Copy)
+
+        t3_stage(0)
+        tab_stage(0)
+        gk16 = sb("gk16", [P, PACK], F32)
+        nc.vector.tensor_scalar(out=gk16[:], in0=gk_sb[:], scalar1=0.0625, scalar2=None, op0=ALU.mult)
         xq_w = sb("xq_w", [P, S], U32)
         xq_s = sb("xq_s", [P, S], U8)
         x2_w = sb("x2_w", [P, S], U32)
-        x2_s = sb("x2_s", [P, S], U8)
         nc.vector.tensor_copy(out=xq_w[:], in_=xw[:].indirect(offs_l[:]))
+        nc.vector.tensor_copy(out=x2_w[:], in_=xw[:].indirect(two_l[:]))
         nc.vector.tensor_copy(out=xq_s[:], in_=xs[:].indirect(offs_l[:]))
         w1_g = sb("w1_g", [P, PACK * H], BF16)
-        for h in range(2):
-            nc.scalar.copy(out=w1_g[:].rearrange("p (t m j) -> p m j t", t=PACK, j=PACK)[:, 64 * h:64 * (h + 1)],
-                           in_=w1_raw[h][:].rearrange("p j (m t) -> p m j t", t=PACK))
+        w1_dst = w1_g[:].rearrange("p (t m j) -> p m j t", t=PACK, j=PACK)
+        w1_src = w1_raw[:].rearrange("p j (m t) -> p m j t", t=PACK)
+        nc.scalar.copy(out=w1_dst[:, 0:64], in_=w1_src[:, 0:64])
+        nc.vector.tensor_copy(out=w1_dst[:, 64:P], in_=w1_src[:, 64:P])
         w1_w, w1_s = quant("w1", w1_g)
         y_ps = [psum.tile([P, S], F32, name="bank%d" % t) for t in range(PACK)]
         for t in range(PACK):
             cols = slice(t * P, (t + 1) * P)
             mx(y_ps[t][:], w1_w[:, cols], w1_s[:, cols], xq_w[:], xq_s[:], True, True)
-        dk_w = sb("dk_w", [P, H], U32, tag="dt0")
-        dk_s = sb("dk_s", [P, H], U8, tag="dt1")
+        dk_s = sb("dk_s", [P, H], U8, tag="dt0")
         key_w = sb("key_w", [P, H], U32)
         key_s = sb("key_s", [P, H], U8)
         nc.vector.tensor_copy(out=dk_s[:], in_=dsc[:].indirect(kidx_l[:]))
         nc.vector.tensor_copy(out=key_s[:].rearrange("p (t m) -> p m t", t=PACK), in_=dk_s[:].rearrange("p (m t) -> p m t", t=PACK))
         for e in range(2):
             nc.sync.dma_start(out=key_s[2 + e:P:32, :].bitcast(I32), in_=key_s[16 + e:P:32, :].bitcast(I32))
-        nc.vector.tensor_copy(out=x2_w[:], in_=xw[:].indirect(two_l[:]))
+        x2_s = sb("x2_s", [P, S], U8, tag="w1_g")
         nc.vector.tensor_copy(out=x2_s[:], in_=xs[:].indirect(two_l[:]))
+        dk_w = sb("dk_w", [P, H], U32, tag="dt1")
         nc.vector.tensor_copy(out=dk_w[:], in_=dw[:].indirect(kidx_l[:]))
         nc.vector.tensor_copy(out=key_w[:].bitcast(I32).rearrange("p (t m) -> p m t", t=PACK), in_=dk_w[:].bitcast(I32).rearrange("p (m t) -> p m t", t=PACK))
         s_ps = [psum.tile([P, S], F32, name="bank%d" % (PACK + t)) for t in range(PACK)]
@@ -126,98 +142,98 @@ def tile_picked_jkeybondkindaharm_none_p_kernel(tc, x_words, x_scales, w1, d_wor
             cols = slice(t * P, (t + 1) * P)
             mx(s_ps[t][:], key_w[:, cols], key_s[:, cols], x2_w[:], x2_s[:], True, True)
 
+        tab_stage(1)
         z_pl = sb("z_pl", [P, PACK, S], BF16)
         dts = []
 
         def z_scale(t):
             nc.vector.tensor_scalar(out=z_pl[:, t, :], in0=dts[t][:], scalar1=gn_sb[:, t:t + 1], scalar2=None, op0=ALU.mult)
 
-        for t in range(PACK):
-            y_sb = sb("y_sb%d" % t, [P, S], F32)
-            nc.scalar.copy(out=y_sb[:], in_=y_ps[t][:])
-            pa = sb("pa%d" % t, [P, W], F32)
-            pb = sb("pb%d" % t, [P, W], F32)
-            nc.scalar.activation(out=pa[:], in_=y_sb[:].indirect(n1_l[:]), func=ACT.Copy)
-            nc.scalar.activation(out=pb[:], in_=y_sb[:].indirect(n2_l[:]), func=ACT.Copy)
-            dt = sb("dt%d" % t, [P, S], F32)
-            nc.vector.tensor_tensor(out=dt[:].indirect(n1_l[:]), in0=pa[:], in1=pb[:], op=ALU.add)
-            if t > 0:
-                z_scale(t - 1)
-            nc.vector.tensor_tensor(out=dt[:].indirect(n2_l[:]), in0=pa[:], in1=pb[:], op=ALU.mult)
-            dts.append(dt)
-        for t in range(PACK):
-            tab_stage(t)
-        st = sb("st", [P, PACK, S], F32)
-        for t in range(PACK):
-            s_sb = sb("s_sb%d" % t, [P, S], F32)
-            nc.scalar.mul(out=s_sb[:], in_=s_ps[t][:], mul=0.0625)
-            s5 = sb("s5_%d" % t, [P, S], F32)
-            for cols, lst in halves(n5_l):
-                nc.scalar.activation(out=s5[:, cols], in_=s_sb[:].indirect(lst), func=ACT.Copy)
-            if t < T3_ON_SCALAR:
-                t3 = sb("t3_%d" % t, [P, S], F32)
-                for cols, lst in halves(n3_l):
-                    nc.scalar.activation(out=t3[:, cols], in_=gtab[t][:].indirect(lst), func=ACT.Copy)
-                nc.vector.tensor_tensor(out=st[:, t, :], in0=t3[:], in1=s5[:], op=ALU.mult)
-            else:
-                for cols, lst in halves(n3_l):
-                    nc.vector.tensor_tensor(out=st[:, t, cols], in0=gtab[t][:].indirect(lst), in1=s5[:, cols], op=ALU.mult)
-            if t == 0:
-                z_scale(PACK - 1)
-        w_g = []
-        for i in range(2):
-            w_g.append(sb("w_g%d" % i, [P, PACK * N], BF16, tag="s_sb%d" % (2 + i)))
-            nc.scalar.copy(out=w_g[i][:].rearrange("p (c i j) -> p c j i", i=4, j=PACK), in_=w_raw[i][:].rearrange("p j (c i) -> p c j i", i=4))
+        for t0 in (0, 2):
+            pair = (t0, t0 + 1)
+            y_sb, pa, pb = {}, {}, {}
+            for t in pair:
+                y_sb[t] = sb("y_sb%d" % t, [P, S], F32, tag=("gtab1", "y_sb1")[t % 2])
+                nc.scalar.copy(out=y_sb[t][:], in_=y_ps[t][:])
+            for t in pair:
+                pa[t] = sb("pa%d" % t, [P, W], F32)
+                nc.scalar.activation(out=pa[t][:], in_=y_sb[t][:].indirect(n1_l[:]), func=ACT.Copy)
+            for t in pair:
+                pb[t] = sb("pb%d" % t, [P, W], F32)
+                nc.scalar.activation(out=pb[t][:], in_=y_sb[t][:].indirect(n2_l[:]), func=ACT.Copy)
+            for t in pair:
+                dts.append(sb("dt%d" % t, [P, S], F32))
+                nc.vector.tensor_tensor(out=dts[t][:].indirect(n1_l[:]), in0=pa[t][:], in1=pb[t][:], op=ALU.add)
+            for t in pair:
+                nc.vector.tensor_tensor(out=dts[t][:].indirect(n2_l[:]), in0=pa[t][:], in1=pb[t][:], op=ALU.mult)
+            for t in pair:
+                z_scale(t)
+        tab_stage(2, "gtab1")
+        tab_stage(3, "y_sb1")
+        t3_stage(1, "gtab1")
+        t3_stage(2, "y_sb1")
+        t3_stage(3, "tab_raw1")
+        def w_cast(name, raw, c0, width, tag, copy=nc.scalar.copy):
+            grouped = sb(name, [P, PACK * width], BF16, tag=tag)
+            copy(out=grouped[:].rearrange("p (c i j) -> p c j i", i=4, j=PACK),
+                 in_=raw[:, :, c0:c0 + width].rearrange("p j (c i) -> p c j i", i=4))
+            return grouped
 
+        st = sb("st", [P, PACK, S], F32)
+        s_sb = [sb("s_sb%d" % t, [P, S], F32) for t in range(PACK)]
+        s5 = sb("s5", [P, PACK, S], F32)
+        z2_g = [sb("z2_g%d" % h, [P, PACK * HALF], BF16) for h in range(2)]
+        z2_w = sb("z2_w", [P, S], U32)
+        z2_s = sb("z2_s", [P, S], U8)
         z_g = sb("z_g", [P, PACK * S], BF16)
         nc.vector.tensor_copy(out=z_g[:].rearrange("p (c i t) -> p c t i", i=4, t=PACK), in_=z_pl[:].rearrange("p t (c i) -> p c t i", i=4))
-        z2_g = sb("z2_g", [P, PACK * S], BF16)
-        nc.vector.tensor_tensor(out=z2_g[:].rearrange("p (c i t) -> p c t i", i=4, t=PACK),
-                                in0=st[:].rearrange("p t (c i) -> p c t i", i=4),
-                                in1=t4[:].rearrange("p t (c i) -> p c t i", i=4), op=ALU.add)
         z_w, z_s = quant("z", z_g)
-        w2_w, w2_s = quant("w2", w_g[0])
-        z2_w, z2_s = quant("z2", z2_g)
-        w3_w, w3_s = quant("w3", w_g[1])
-
-        h_ps = [psum.tile([P, S], F32, name="bank%d" % mt) for mt in range(PACK)]
+        w2_g = [w_cast("w2_g0", w_raw[0], 0, HALF, "tab_raw2"), w_cast("w2_g1", w_raw[0], HALF, HALF, "dt3", nc.vector.tensor_copy)]
+        w2_q = [quant("w2_%d" % h, w2_g[h], HALF) for h in range(2)]
+        for h in range(2):
+            cols, n5_h = halves(n5_l)[h]
+            n3_h = halves(n3_l)[h][1]
+            for t in range(PACK):
+                if h == 0:
+                    nc.scalar.activation(out=s_sb[t][:], in_=s_ps[t][:], func=ACT.Copy, scale=gk16[:, t:t + 1])
+                nc.scalar.activation(out=s5[:, t, cols], in_=s_sb[t][:].indirect(n5_h), func=ACT.Copy)
+                if t < T3_ON_SCALAR:
+                    nc.vector.tensor_tensor(out=st[:, t, cols], in0=t3[t][:, cols], in1=s5[:, t, cols], op=ALU.mult)
+                else:
+                    nc.vector.tensor_tensor(out=st[:, t, cols], in0=tab_raw[t][:].indirect(n3_h), in1=s5[:, t, cols], op=ALU.mult)
+            nc.vector.tensor_tensor(out=z2_g[h][:].rearrange("p (c i t) -> p c t i", i=4, t=PACK),
+                                    in0=st[:, :, cols].rearrange("p t (c i) -> p c t i", i=4),
+                                    in1=t4[:, :, cols].rearrange("p t (c i) -> p c t i", i=4), op=ALU.add)
+            nc.vector.quantize_mx(out=z2_w[:, cols].bitcast(FP8X4), scales=z2_s[:, cols], in_=z2_g[h][:])
+        w3_g = [w_cast("w3_g%d" % mt, w_raw[1], mt * P, P, "s_sb%d" % mt) for mt in range(PACK)]
+        w3_q = [quant("w3_%d" % mt, w3_g[mt], P) for mt in range(PACK)]
+        h_ps = [psum.tile([P, S], F32, name="bank%d" % (PACK + mt)) for mt in range(PACK)]
         for mt in range(PACK):
-            cols = slice(mt * P, (mt + 1) * P)
-            mx(h_ps[mt][:], w2_w[:, cols], w2_s[:, cols], z_w[:], z_s[:], True, False)
+            cols = slice((mt % 2) * P, (mt % 2 + 1) * P)
+            mx(h_ps[mt][:], w2_q[mt // 2][0][:, cols], w2_q[mt // 2][1][:, cols], z_w[:], z_s[:], True, False)
         for mt in range(PACK):
-            cols = slice(mt * P, (mt + 1) * P)
-            mx(h_ps[mt][:], w3_w[:, cols], w3_s[:, cols], z2_w[:], z2_s[:], False, True)
-        h_sb = [sb("h_sb%d" % mt, [P, S], F32, tag="y_sb%d" % mt) for mt in range(PACK)]
-        hh = [sb("hh%d" % mt, [P, S], F32, tag="s_sb%d" % mt) for mt in range(PACK)]
-        pa2 = [sb("pa2_%d" % mt, [P, S], F32, tag="dt%d" % mt) for mt in range(PACK)]
-        pp = [sb("pp%d" % mt, [P, S], F32, tag="s5_%d" % mt) for mt in range(PACK)]
-        num = [sb("num%d" % mt, [P, S], F32, tag="gtab%d" % mt) for mt in range(PACK)]
+            mx(h_ps[mt][:], w3_q[mt][0][:], w3_q[mt][1][:], z2_w[:], z2_s[:], False, True)
+        h_sb = [sb("h_sb%d" % mt, [P, S], F32) for mt in range(PACK)]
+        hh = [sb("hh%d" % mt, [P, S], F32) for mt in range(PACK)]
+        pa2 = [sb("pa2_%d" % mt, [P, S], F32) for mt in range(PACK)]
+        pp = [sb("pp%d" % mt, [P, S], F32) for mt in range(PACK)]
         ssq = [sb("ssq%d" % mt, [P, S], F32, tag="tab_raw%d" % mt) for mt in range(PACK)]
         root = [sb("root%d" % mt, [P, S], F32) for mt in range(PACK)]
         rec = [sb("rec%d" % mt, [P, S], F32) for mt in range(PACK)]
         res = [sb("res%d" % mt, [P, S], F32) for mt in range(PACK)]
 
-        def stage_a(mt):
+        for mt in range(PACK):
             nc.scalar.copy(out=h_sb[mt][:], in_=h_ps[mt][:])
-            nc.scalar.activation(out=hh[mt][:], in_=h_ps[mt][:], func=ACT.Square)
             for c2, lst in halves(n6_l):
                 nc.vector.tensor_copy(out=pa2[mt][:, c2], in_=h_sb[mt][:].indirect(lst))
-
-        def stage_b(mt):
+        for mt in range(PACK):
+            nc.scalar.activation(out=hh[mt][:], in_=h_ps[mt][:], func=ACT.Square)
             nc.scalar.activation(out=pp[mt][:], in_=pa2[mt][:], func=ACT.Square)
-            nc.vector.tensor_tensor(out=num[mt][:], in0=h_sb[mt][:], in1=pa2[mt][:], op=ALU.mult)
             nc.vector.scalar_tensor_tensor(out=ssq[mt][:], in0=pp[mt][:], scalar=0.5, in1=hh[mt][:], op0=ALU.add, op1=ALU.add)
-
-        def stage_c(mt):
+        for mt in range(PACK):
             nc.scalar.activation(out=root[mt][:], in_=ssq[mt][:], func=ACT.Abs_reciprocal_sqrt)
             nc.scalar.activation(out=rec[mt][:], in_=root[mt][:], func=ACT.Square)
-            nc.vector.scalar_tensor_tensor(out=res[mt][:], in0=num[mt][:], scalar=2.0, in1=rec[mt][:], op0=ALU.mult, op1=ALU.mult)
+            num = sb("num%d" % mt, [P, S], F32, tag="tab_raw%d" % mt)
+            nc.vector.tensor_tensor(out=num[:], in0=h_sb[mt][:], in1=pa2[mt][:], op=ALU.mult)
+            nc.vector.scalar_tensor_tensor(out=res[mt][:], in0=num[:], scalar=2.0, in1=rec[mt][:], op0=ALU.mult, op1=ALU.mult)
             nc.sync.dma_start(out=out[mt * P:(mt + 1) * P, :], in_=res[mt][:])
-
-        for step in range(PACK + 2):
-            if step < PACK:
-                stage_a(step)
-            if 1 <= step <= PACK:
-                stage_b(step - 1)
-            if step >= 2:
-                stage_c(step - 2)

@@ -49,16 +49,18 @@ def tile_picked_jkeybondkindaharm_none_p_kernel(tc, x_words, x_scales, w1, d_wor
 
         xs = sb("xs", [P, T], U8)
         dsc = sb("dsc", [P, G], U8)
+        nc.vector.memset(xs[:].bitcast(I32), 0)
         warm_in = sb("warm_in", [P, 1], F32)
         warm_out = sb("warm_out", [P, 1], F32)
         nc.vector.memset(warm_in[:], 1.0)
         nc.scalar.activation(out=warm_out[:], in_=warm_in[:], func=ACT.Abs_reciprocal_sqrt)
-        nc.vector.memset(xs[:].bitcast(I32), 0)
-        nc.vector.memset(dsc[:].bitcast(I32), 0)
+        nc.gpsimd.memset(dsc[:].bitcast(I32), 0)
+        key_s = sb("key_s", [P, H], U8)
+        nc.vector.memset(key_s[:].bitcast(I32), 0)
         gk_sb = sb("gk_sb", [P, PACK], F32)
         nc.sync.dma_start(out=gk_sb[:], in_=gk.rearrange("(p t) o -> p (t o)", t=PACK))
         tab_rows = tab.rearrange("(p t) c -> p t c", t=PACK)
-        tab_raw = [sb("tab_raw%d" % t, [P, J], F32) for t in range(PACK)]
+        tab_raw = {t: sb("tab_raw%d" % t, [P, J], F32) for t in range(2)}
         nc.sync.dma_start(out=tab_raw[0][:], in_=tab_rows[:, 0, :])
         n4_l = load_list("n4_l", n4)
         n3_l = load_list("n3_l", n3)
@@ -76,17 +78,10 @@ def tile_picked_jkeybondkindaharm_none_p_kernel(tc, x_words, x_scales, w1, d_wor
         nc.sync.dma_start(out=dw[:].bitcast(I32), in_=d_words[0].rearrange("p n r -> p (n r)").bitcast(I32))
         n1_l = load_list("n1_l", n1)
         n2_l = load_list("n2_l", n2)
-        d_rows = d_scales[0].rearrange("(g e) c -> e g c", e=2)
-        for e in range(2):
-            nc.sync.dma_start(out=dsc[e:P:16, :].bitcast(I32), in_=d_rows[e].bitcast(I32))
-        for t in (2, 3):
-            nc.sync.dma_start(out=tab_raw[t][:], in_=tab_rows[:, t, :])
+        nc.sync.dma_start(out=dsc[0:P:8, :].bitcast(I32), in_=d_scales[0].bitcast(I32))
         n5_l = load_list("n5_l", n5)
         gn_sb = sb("gn_sb", [P, PACK], F32)
         nc.sync.dma_start(out=gn_sb[:], in_=gn.rearrange("(p t) o -> p (t o)", t=PACK))
-        w_raw = [sb("w_raw%d" % i, [P, PACK, N], F32) for i in range(2)]
-        for i, w in enumerate((w2, w3)):
-            nc.sync.dma_start(out=w_raw[i][:], in_=w.rearrange("(p j) c -> p j c", j=PACK))
         n6_l = load_list("n6_l", n6)
 
         gtab = {}
@@ -118,31 +113,41 @@ def tile_picked_jkeybondkindaharm_none_p_kernel(tc, x_words, x_scales, w1, d_wor
         w1_g = sb("w1_g", [P, PACK * H], BF16)
         w1_dst = w1_g[:].rearrange("p (t m j) -> p m j t", t=PACK, j=PACK)
         w1_src = w1_raw[:].rearrange("p j (m t) -> p m j t", t=PACK)
-        nc.scalar.copy(out=w1_dst[:, 0:64], in_=w1_src[:, 0:64])
-        nc.vector.tensor_copy(out=w1_dst[:, 64:P], in_=w1_src[:, 64:P])
+        nc.scalar.copy(out=w1_dst[:, 0:40], in_=w1_src[:, 0:40])
+        nc.vector.tensor_copy(out=w1_dst[:, 40:P], in_=w1_src[:, 40:P])
         w1_w, w1_s = quant("w1", w1_g)
+        for t, tag in ((3, "tab_raw0"), (2, "gtab0")):
+            tab_raw[t] = sb("tab_raw%d" % t, [P, J], F32, tag=tag)
+            nc.sync.dma_start(out=tab_raw[t][:], in_=tab_rows[:, t, :])
+        w_raw = []
+        for name, w, tag in (("w2_raw", w2, "xw"), ("w3_raw", w3, "w1_raw")):
+            w_raw.append(sb(name, [P, PACK, N], F32, tag=tag))
+            nc.sync.dma_start(out=w_raw[-1][:], in_=w.rearrange("(p j) c -> p j c", j=PACK))
         y_ps = [psum.tile([P, S], F32, name="bank%d" % t) for t in range(PACK)]
         for t in range(PACK):
             cols = slice(t * P, (t + 1) * P)
             mx(y_ps[t][:], w1_w[:, cols], w1_s[:, cols], xq_w[:], xq_s[:], True, True)
-        dk_s = sb("dk_s", [P, H], U8, tag="dt0")
-        key_w = sb("key_w", [P, H], U32)
-        key_s = sb("key_s", [P, H], U8)
-        nc.vector.tensor_copy(out=dk_s[:], in_=dsc[:].indirect(kidx_l[:]))
-        nc.vector.tensor_copy(out=key_s[:].rearrange("p (t m) -> p m t", t=PACK), in_=dk_s[:].rearrange("p (m t) -> p m t", t=PACK))
-        for e in range(2):
-            nc.sync.dma_start(out=key_s[2 + e:P:32, :].bitcast(I32), in_=key_s[16 + e:P:32, :].bitcast(I32))
         x2_s = sb("x2_s", [P, S], U8, tag="w1_g")
         nc.vector.tensor_copy(out=x2_s[:], in_=xs[:].indirect(two_l[:]))
-        dk_w = sb("dk_w", [P, H], U32, tag="dt1")
+        dk_w = sb("dk_w", [P, H], U32, tag="dt0")
+        key_w = sb("key_w", [P, H], U32)
         nc.vector.tensor_copy(out=dk_w[:], in_=dw[:].indirect(kidx_l[:]))
         nc.vector.tensor_copy(out=key_w[:].bitcast(I32).rearrange("p (t m) -> p m t", t=PACK), in_=dk_w[:].bitcast(I32).rearrange("p (m t) -> p m t", t=PACK))
+        dealt_s = sb("dealt_s", [P, H], U8)
+        dk_s = [sb("dk_s%d" % h, [P, HALF], U8, tag="dt%d" % h) for h in range(2)]
+        for h in (1, 0):
+            nc.vector.tensor_copy(out=dk_s[h][:], in_=dsc[:].indirect(halves(kidx_l)[h][1]))
+        for h in (1, 0):
+            nc.vector.tensor_copy(out=dealt_s[:].rearrange("p (t m) -> p m t", t=PACK)[:, 64 * h:64 * (h + 1)], in_=dk_s[h][:].rearrange("p (m t) -> p m t", t=PACK))
+        for q in range(4):
+            nc.sync.dma_start(out=key_s[32 * q:32 * q + 4, :].bitcast(I32), in_=dealt_s[32 * q:32 * q + 32:8, :].bitcast(I32))
         s_ps = [psum.tile([P, S], F32, name="bank%d" % (PACK + t)) for t in range(PACK)]
         for t in range(PACK):
             cols = slice(t * P, (t + 1) * P)
             mx(s_ps[t][:], key_w[:, cols], key_s[:, cols], x2_w[:], x2_s[:], True, True)
 
         tab_stage(1)
+        t3_stage(1)
         z_pl = sb("z_pl", [P, PACK, S], BF16)
         dts = []
 
@@ -153,7 +158,7 @@ def tile_picked_jkeybondkindaharm_none_p_kernel(tc, x_words, x_scales, w1, d_wor
             pair = (t0, t0 + 1)
             y_sb, pa, pb = {}, {}, {}
             for t in pair:
-                y_sb[t] = sb("y_sb%d" % t, [P, S], F32, tag=("gtab1", "y_sb1")[t % 2])
+                y_sb[t] = sb("y_sb%d" % t, [P, S], F32, tag=("tab_raw1", "gtab1")[t % 2])
                 nc.scalar.copy(out=y_sb[t][:], in_=y_ps[t][:])
             for t in pair:
                 pa[t] = sb("pa%d" % t, [P, W], F32)
@@ -168,11 +173,11 @@ def tile_picked_jkeybondkindaharm_none_p_kernel(tc, x_words, x_scales, w1, d_wor
                 nc.vector.tensor_tensor(out=dts[t][:].indirect(n2_l[:]), in0=pa[t][:], in1=pb[t][:], op=ALU.mult)
             for t in pair:
                 z_scale(t)
-        tab_stage(2, "gtab1")
-        tab_stage(3, "y_sb1")
-        t3_stage(1, "gtab1")
-        t3_stage(2, "y_sb1")
-        t3_stage(3, "tab_raw1")
+        tab_stage(2, "tab_raw1")
+        tab_stage(3, "gtab1")
+        t3_stage(2, "tab_raw1")
+        t3_stage(3, "gtab1")
+
         def w_cast(name, raw, c0, width, tag, copy=nc.scalar.copy):
             grouped = sb(name, [P, PACK * width], BF16, tag=tag)
             copy(out=grouped[:].rearrange("p (c i j) -> p c j i", i=4, j=PACK),
@@ -188,7 +193,7 @@ def tile_picked_jkeybondkindaharm_none_p_kernel(tc, x_words, x_scales, w1, d_wor
         z_g = sb("z_g", [P, PACK * S], BF16)
         nc.vector.tensor_copy(out=z_g[:].rearrange("p (c i t) -> p c t i", i=4, t=PACK), in_=z_pl[:].rearrange("p t (c i) -> p c t i", i=4))
         z_w, z_s = quant("z", z_g)
-        w2_g = [w_cast("w2_g0", w_raw[0], 0, HALF, "tab_raw2"), w_cast("w2_g1", w_raw[0], HALF, HALF, "dt3", nc.vector.tensor_copy)]
+        w2_g = [w_cast("w2_g%d" % h, w_raw[0], h * HALF, HALF, ("gtab0", "tab_raw0")[h]) for h in range(2)]
         w2_q = [quant("w2_%d" % h, w2_g[h], HALF) for h in range(2)]
         for h in range(2):
             cols, n5_h = halves(n5_l)[h]
@@ -217,7 +222,7 @@ def tile_picked_jkeybondkindaharm_none_p_kernel(tc, x_words, x_scales, w1, d_wor
         hh = [sb("hh%d" % mt, [P, S], F32) for mt in range(PACK)]
         pa2 = [sb("pa2_%d" % mt, [P, S], F32) for mt in range(PACK)]
         pp = [sb("pp%d" % mt, [P, S], F32) for mt in range(PACK)]
-        ssq = [sb("ssq%d" % mt, [P, S], F32, tag="tab_raw%d" % mt) for mt in range(PACK)]
+        ssq = [sb("ssq%d" % mt, [P, S], F32) for mt in range(PACK)]
         root = [sb("root%d" % mt, [P, S], F32) for mt in range(PACK)]
         rec = [sb("rec%d" % mt, [P, S], F32) for mt in range(PACK)]
         res = [sb("res%d" % mt, [P, S], F32) for mt in range(PACK)]
@@ -233,7 +238,7 @@ def tile_picked_jkeybondkindaharm_none_p_kernel(tc, x_words, x_scales, w1, d_wor
         for mt in range(PACK):
             nc.scalar.activation(out=root[mt][:], in_=ssq[mt][:], func=ACT.Abs_reciprocal_sqrt)
             nc.scalar.activation(out=rec[mt][:], in_=root[mt][:], func=ACT.Square)
-            num = sb("num%d" % mt, [P, S], F32, tag="tab_raw%d" % mt)
+            num = sb("num%d" % mt, [P, S], F32, tag="ssq%d" % mt)
             nc.vector.tensor_tensor(out=num[:], in0=h_sb[mt][:], in1=pa2[mt][:], op=ALU.mult)
             nc.vector.scalar_tensor_tensor(out=res[mt][:], in0=num[:], scalar=2.0, in1=rec[mt][:], op0=ALU.mult, op1=ALU.mult)
             nc.sync.dma_start(out=out[mt * P:(mt + 1) * P, :], in_=res[mt][:])

from contextlib import ExitStack

import concourse.mybir as mybir

K, T, S, N, H, G, W, J = 512, 1024, 512, 512, 512, 2048, 256, 512
FLOPS = 4 * 2 * 512 * 512 * 512

F32 = mybir.dt.float32
BF16 = mybir.dt.bfloat16
I32 = mybir.dt.int32
U32 = mybir.dt.uint32
U16 = mybir.dt.uint16
U8 = mybir.dt.uint8
FP8X4 = mybir.dt.float8_e4m3fn_x4
ALU = mybir.AluOpType
ACT = mybir.ActivationFunctionType
P = 128
PACK = 4
HALF = 256
T3_ON_SCALAR = 4


def tile_picked_jkeybondkindaharm_none_p_kernel(tc, x_words, x_scales, w1, d_words, d_scales, tab, gn, gk, w2, w3, offs, kidx, two, n1, n2, n3, n4, n5, n6, out):
    nc = tc.nc
    with ExitStack() as ctx:
        lists = ctx.enter_context(tc.tile_pool(name="lists", bufs=1))
        keep = ctx.enter_context(tc.tile_pool(name="keep", bufs=1))
        psum = ctx.enter_context(tc.psum_pool(name="psum", bufs=1))

        def load_list(name, src):
            tl = lists.tile(list(src.shape), U16, name=name)
            nc.sync.dma_start(out=tl[:], in_=src)
            return tl

        def sb(name, shape, dtype, tag=None):
            return keep.tile(shape, dtype, name=name, tag=tag or name, align_bytes=64)

        def halves(lst):
            return [(slice(h * HALF, (h + 1) * HALF), lst[:, h * 16:(h + 1) * 16]) for h in range(2)]

        def mx(acc, lw, ls, rw, rs, start, stop):
            nc.tensor.matmul_mx(out=acc, lhsT=lw.bitcast(FP8X4), lhsT_scale=ls, rhs=rw.bitcast(FP8X4), rhs_scale=rs, start=start, stop=stop)

        def quant(name, grouped, width=512, tag=None):
            words = sb(name + "_w", [P, width], U32, tag=tag)
            scales = sb(name + "_s", [P, width], U8)
            nc.vector.quantize_mx(out=words[:].bitcast(FP8X4), scales=scales[:], in_=grouped[:])
            return words, scales

        xs = sb("xs", [P, T], U8)
        dsc = sb("dsc", [P, G], U8)
        nc.vector.memset(xs[:].bitcast(I32), 0)
        warm_in = sb("warm_in", [P, 1], F32)
        warm_out = sb("warm_out", [P, 1], F32)
        nc.vector.memset(warm_in[:], 1.0)
        nc.scalar.activation(out=warm_out[:], in_=warm_in[:], func=ACT.Abs_reciprocal_sqrt)
        nc.gpsimd.memset(dsc[:].bitcast(I32), 0)
        key_s = sb("key_s", [P, H], U8)
        nc.vector.memset(key_s[:].bitcast(I32), 0)
        gk_sb = sb("gk_sb", [P, PACK], F32)
        nc.sync.dma_start(out=gk_sb[:], in_=gk.rearrange("(p t) o -> p (t o)", t=PACK))
        tab_rows = tab.rearrange("(p t) c -> p t c", t=PACK)
        tab_raw = {t: sb("tab_raw%d" % t, [P, J], F32) for t in range(2)}
        nc.sync.dma_start(out=tab_raw[0][:], in_=tab_rows[:, 0, :])
        n4_l = load_list("n4_l", n4)
        n3_l = load_list("n3_l", n3)
        offs_l = load_list("offs_l", offs)
        xw = sb("xw", [P, T], U32)
        nc.sync.dma_start(out=xw[:].bitcast(I32), in_=x_words[0].rearrange("p n r -> p (n r)").bitcast(I32))
        two_l = load_list("two_l", two)
        w1_raw = sb("w1_raw", [P, PACK, H], F32)
        nc.sync.dma_start(out=w1_raw[:], in_=w1.rearrange("(p j) c -> p j c", j=PACK))
        for q in range(4):
            nc.sync.dma_start(out=xs[32 * q:32 * q + 4, :].bitcast(I32), in_=x_scales[0, 4 * q:4 * q + 4, :].bitcast(I32))
        kidx_l = load_list("kidx_l", kidx)
        nc.sync.dma_start(out=tab_raw[1][:], in_=tab_rows[:, 1, :])
        dw = sb("dw", [P, G], U32)
        nc.sync.dma_start(out=dw[:].bitcast(I32), in_=d_words[0].rearrange("p n r -> p (n r)").bitcast(I32))
        n1_l = load_list("n1_l", n1)
        n2_l = load_list("n2_l", n2)
        nc.sync.dma_start(out=dsc[0:P:8, :].bitcast(I32), in_=d_scales[0].bitcast(I32))
        n5_l = load_list("n5_l", n5)
        gn_sb = sb("gn_sb", [P, PACK], F32)
        nc.sync.dma_start(out=gn_sb[:], in_=gn.rearrange("(p t) o -> p (t o)", t=PACK))
        n6_l = load_list("n6_l", n6)

        gtab = {}
        t4 = sb("t4", [P, PACK, S], F32)
        t3 = {}

        def tab_stage(t, tag=None):
            gtab[t] = sb("gtab%d" % t, [P, J], F32, tag=tag)
            nc.scalar.activation(out=gtab[t][:], in_=tab_raw[t][:], func=ACT.Copy, scale=gk_sb[:, t:t + 1])
            for cols, lst in halves(n4_l):
                nc.scalar.activation(out=t4[:, t, cols], in_=gtab[t][:].indirect(lst), func=ACT.Copy)

        def t3_stage(t, tag=None):
            if t < T3_ON_SCALAR:
                t3[t] = sb("t3_%d" % t, [P, S], F32, tag=tag)
                for cols, lst in halves(n3_l):
                    nc.scalar.activation(out=t3[t][:, cols], in_=tab_raw[t][:].indirect(lst), func=ACT.Copy)

        t3_stage(0)
        tab_stage(0)
        gk16 = sb("gk16", [P, PACK], F32)
        nc.vector.tensor_scalar(out=gk16[:], in0=gk_sb[:], scalar1=0.0625, scalar2=None, op0=ALU.mult)
        xq_w = sb("xq_w", [P, S], U32)
        xq_s = sb("xq_s", [P, S], U8)
        x2_w = sb("x2_w", [P, S], U32)
        nc.vector.tensor_copy(out=xq_w[:], in_=xw[:].indirect(offs_l[:]))
        nc.vector.tensor_copy(out=x2_w[:], in_=xw[:].indirect(two_l[:]))
        nc.vector.tensor_copy(out=xq_s[:], in_=xs[:].indirect(offs_l[:]))
        w1_g = sb("w1_g", [P, PACK * H], BF16)
        w1_dst = w1_g[:].rearrange("p (t m j) -> p m j t", t=PACK, j=PACK)
        w1_src = w1_raw[:].rearrange("p j (m t) -> p m j t", t=PACK)
        nc.scalar.copy(out=w1_dst[:, 0:40], in_=w1_src[:, 0:40])
        nc.vector.tensor_copy(out=w1_dst[:, 40:P], in_=w1_src[:, 40:P])
        w1_w, w1_s = quant("w1", w1_g)
        for t, tag in ((3, "tab_raw0"), (2, "gtab0")):
            tab_raw[t] = sb("tab_raw%d" % t, [P, J], F32, tag=tag)
            nc.sync.dma_start(out=tab_raw[t][:], in_=tab_rows[:, t, :])
        w_raw = []
        for name, w, tag in (("w2_raw", w2, "xw"), ("w3_raw", w3, "w1_raw")):
            w_raw.append(sb(name, [P, PACK, N], F32, tag=tag))
            nc.sync.dma_start(out=w_raw[-1][:], in_=w.rearrange("(p j) c -> p j c", j=PACK))
        y_ps = [psum.tile([P, S], F32, name="bank%d" % t) for t in range(PACK)]
        for t in range(PACK):
            cols = slice(t * P, (t + 1) * P)
            mx(y_ps[t][:], w1_w[:, cols], w1_s[:, cols], xq_w[:], xq_s[:], True, True)
        x2_s = sb("x2_s", [P, S], U8, tag="w1_g")
        nc.vector.tensor_copy(out=x2_s[:], in_=xs[:].indirect(two_l[:]))
        dk_w = sb("dk_w", [P, H], U32, tag="dt0")
        key_w = sb("key_w", [P, H], U32)
        nc.vector.tensor_copy(out=dk_w[:], in_=dw[:].indirect(kidx_l[:]))
        nc.vector.tensor_copy(out=key_w[:].bitcast(I32).rearrange("p (t m) -> p m t", t=PACK), in_=dk_w[:].bitcast(I32).rearrange("p (m t) -> p m t", t=PACK))
        dealt_s = sb("dealt_s", [P, H], U8)
        dk_s = [sb("dk_s%d" % h, [P, HALF], U8, tag="dt%d" % h) for h in range(2)]
        for h in (1, 0):
            nc.vector.tensor_copy(out=dk_s[h][:], in_=dsc[:].indirect(halves(kidx_l)[h][1]))
        for h in (1, 0):
            nc.vector.tensor_copy(out=dealt_s[:].rearrange("p (t m) -> p m t", t=PACK)[:, 64 * h:64 * (h + 1)], in_=dk_s[h][:].rearrange("p (m t) -> p m t", t=PACK))
        for q in range(4):
            nc.sync.dma_start(out=key_s[32 * q:32 * q + 4, :].bitcast(I32), in_=dealt_s[32 * q:32 * q + 32:8, :].bitcast(I32))
        s_ps = [psum.tile([P, S], F32, name="bank%d" % (PACK + t)) for t in range(PACK)]
        for t in range(PACK):
            cols = slice(t * P, (t + 1) * P)
            mx(s_ps[t][:], key_w[:, cols], key_s[:, cols], x2_w[:], x2_s[:], True, True)

        tab_stage(1)
        t3_stage(1)
        z_pl = sb("z_pl", [P, PACK, S], BF16)
        dts = []

        def z_scale(t):
            nc.vector.tensor_scalar(out=z_pl[:, t, :], in0=dts[t][:], scalar1=gn_sb[:, t:t + 1], scalar2=None, op0=ALU.mult)

        for t0 in (0, 2):
            pair = (t0, t0 + 1)
            y_sb, pa, pb = {}, {}, {}
            for t in pair:
                y_sb[t] = sb("y_sb%d" % t, [P, S], F32, tag=("tab_raw1", "gtab1")[t % 2])
                nc.scalar.copy(out=y_sb[t][:], in_=y_ps[t][:])
            for t in pair:
                pa[t] = sb("pa%d" % t, [P, W], F32)
                nc.scalar.activation(out=pa[t][:], in_=y_sb[t][:].indirect(n1_l[:]), func=ACT.Copy)
            for t in pair:
                pb[t] = sb("pb%d" % t, [P, W], F32)
                nc.scalar.activation(out=pb[t][:], in_=y_sb[t][:].indirect(n2_l[:]), func=ACT.Copy)
            for t in pair:
                dts.append(sb("dt%d" % t, [P, S], F32))
                nc.vector.tensor_tensor(out=dts[t][:].indirect(n1_l[:]), in0=pa[t][:], in1=pb[t][:], op=ALU.add)
            for t in pair:
                nc.vector.tensor_tensor(out=dts[t][:].indirect(n2_l[:]), in0=pa[t][:], in1=pb[t][:], op=ALU.mult)
            for t in pair:
                z_scale(t)
        tab_stage(2, "tab_raw1")
        tab_stage(3, "gtab1")
        t3_stage(2, "tab_raw1")
        t3_stage(3, "gtab1")

        def w_cast(name, raw, c0, width, tag, copy=nc.scalar.copy):
            grouped = sb(name, [P, PACK * width], BF16, tag=tag)
            copy(out=grouped[:].rearrange("p (c i j) -> p c j i", i=4, j=PACK),
                 in_=raw[:, :, c0:c0 + width].rearrange("p j (c i) -> p c j i", i=4))
            return grouped

        st = sb("st", [P, PACK, S], F32)
        s_sb = [sb("s_sb%d" % t, [P, S], F32) for t in range(PACK)]
        s5 = sb("s5", [P, PACK, S], F32)
        z2_g = [sb("z2_g%d" % h, [P, PACK * HALF], BF16) for h in range(2)]
        z2_w = sb("z2_w", [P, S], U32)
        z2_s = sb("z2_s", [P, S], U8)
        z_g = sb("z_g", [P, PACK * S], BF16)
        nc.vector.tensor_copy(out=z_g[:].rearrange("p (c i t) -> p c t i", i=4, t=PACK), in_=z_pl[:].rearrange("p t (c i) -> p c t i", i=4))
        z_w, z_s = quant("z", z_g)
        w2_g = [w_cast("w2_g%d" % h, w_raw[0], h * HALF, HALF, ("gtab0", "tab_raw0")[h]) for h in range(2)]
        w2_q = [quant("w2_%d" % h, w2_g[h], HALF) for h in range(2)]
        for h in range(2):
            cols, n5_h = halves(n5_l)[h]
            n3_h = halves(n3_l)[h][1]
            for t in range(PACK):
                if h == 0:
                    nc.scalar.activation(out=s_sb[t][:], in_=s_ps[t][:], func=ACT.Copy, scale=gk16[:, t:t + 1])
                nc.scalar.activation(out=s5[:, t, cols], in_=s_sb[t][:].indirect(n5_h), func=ACT.Copy)
                if t < T3_ON_SCALAR:
                    nc.vector.tensor_tensor(out=st[:, t, cols], in0=t3[t][:, cols], in1=s5[:, t, cols], op=ALU.mult)
                else:
                    nc.vector.tensor_tensor(out=st[:, t, cols], in0=tab_raw[t][:].indirect(n3_h), in1=s5[:, t, cols], op=ALU.mult)
            nc.vector.tensor_tensor(out=z2_g[h][:].rearrange("p (c i t) -> p c t i", i=4, t=PACK),
                                    in0=st[:, :, cols].rearrange("p t (c i) -> p c t i", i=4),
                                    in1=t4[:, :, cols].rearrange("p t (c i) -> p c t i", i=4), op=ALU.add)
            nc.vector.quantize_mx(out=z2_w[:, cols].bitcast(FP8X4), scales=z2_s[:, cols], in_=z2_g[h][:])
        w3_g = [w_cast("w3_g%d" % mt, w_raw[1], mt * P, P, "s_sb%d" % mt) for mt in range(PACK)]
        w3_q = [quant("w3_%d" % mt, w3_g[mt], P) for mt in range(PACK)]
        h_ps = [psum.tile([P, S], F32, name="bank%d" % (PACK + mt)) for mt in range(PACK)]
        for mt in range(PACK):
            cols = slice((mt % 2) * P, (mt % 2 + 1) * P)
            mx(h_ps[mt][:], w2_q[mt // 2][0][:, cols], w2_q[mt // 2][1][:, cols], z_w[:], z_s[:], True, False)
        for mt in range(PACK):
            mx(h_ps[mt][:], w3_q[mt][0][:], w3_q[mt][1][:], z2_w[:], z2_s[:], False, True)
        h_sb = [sb("h_sb%d" % mt, [P, S], F32) for mt in range(PACK)]
        hh = [sb("hh%d" % mt, [P, S], F32) for mt in range(PACK)]
        pa2 = [sb("pa2_%d" % mt, [P, S], F32) for mt in range(PACK)]
        pp = [sb("pp%d" % mt, [P, S], F32) for mt in range(PACK)]
        ssq = [sb("ssq%d" % mt, [P, S], F32) for mt in range(PACK)]
        root = [sb("root%d" % mt, [P, S], F32) for mt in range(PACK)]
        rec = [sb("rec%d" % mt, [P, S], F32) for mt in range(PACK)]
        res = [sb("res%d" % mt, [P, S], F32) for mt in range(PACK)]

        for mt in range(PACK):
            nc.scalar.copy(out=h_sb[mt][:], in_=h_ps[mt][:])
            for c2, lst in halves(n6_l):
                nc.vector.tensor_copy(out=pa2[mt][:, c2], in_=h_sb[mt][:].indirect(lst))
        for mt in range(PACK):
            nc.scalar.activation(out=hh[mt][:], in_=h_ps[mt][:], func=ACT.Square)
            nc.scalar.activation(out=pp[mt][:], in_=pa2[mt][:], func=ACT.Square)
            nc.vector.scalar_tensor_tensor(out=ssq[mt][:], in0=pp[mt][:], scalar=0.5, in1=hh[mt][:], op0=ALU.add, op1=ALU.add)
        for mt in range(PACK):
            nc.scalar.activation(out=root[mt][:], in_=ssq[mt][:], func=ACT.Abs_reciprocal_sqrt)
            nc.scalar.activation(out=rec[mt][:], in_=root[mt][:], func=ACT.Square)
            num = sb("num%d" % mt, [P, S], F32, tag="ssq%d" % mt)
            nc.vector.tensor_tensor(out=num[:], in0=h_sb[mt][:], in1=pa2[mt][:], op=ALU.mult)
            nc.vector.scalar_tensor_tensor(out=res[mt][:], in0=num[:], scalar=2.0, in1=rec[mt][:], op0=ALU.mult, op1=ALU.mult)
            nc.sync.dma_start(out=out[mt * P:(mt + 1) * P, :], in_=res[mt][:])
